import numpy as np
import ml_dtypes


def mxq(x, axis, fmt="e4m3"):
    dtype, down = {"e4m3": (ml_dtypes.float8_e4m3fn, 7), "e5m2": (ml_dtypes.float8_e5m2, 14)}[fmt]
    v = np.moveaxis(np.asarray(x, np.float32).astype(ml_dtypes.bfloat16).astype(np.float64), axis, -1)
    blocks = v.reshape(v.shape[:-1] + (-1, 32))
    amax = np.abs(blocks).max(-1, keepdims=True)
    byte = np.maximum(np.where(amax > 0, np.frexp(amax)[1] - 1 + 127, 0) - down, 1)
    scale = np.exp2(byte - 127.0)
    codes = (blocks / scale).astype(np.float32).astype(dtype).astype(np.float64)
    return np.moveaxis((codes * scale).reshape(v.shape), -1, axis)


WIDE = False


def mx_kscale(k):
    if not WIDE:
        return np.ones(k)
    levels = np.array([10, -10, 5, -5, 0])
    if k % 512:
        return np.exp2(np.random.permutation(np.resize(levels, k // 32))).repeat(32)
    a = np.empty((k // 512, 16))
    for p in range(k // 512):
        a[p, :8] = np.random.permutation(np.resize(levels, 8))
        for g in range(8):
            far = levels[np.abs(levels - a[p, g]) >= 10]
            a[p, g + 8] = far[np.random.randint(len(far))]
    return np.exp2(a.ravel()).repeat(32)


BF16 = ml_dtypes.bfloat16


def bf(x):
    return np.asarray(x, np.float32).astype(BF16)


def f64(x):
    return np.asarray(x).astype(np.float64)


E2M1 = np.array([0.0, 0.5, 1.0, 1.5, 2.0, 3.0, 4.0, 6.0, -0.0, -0.5, -1.0, -1.5, -2.0, -3.0, -4.0, -6.0])


def pack_weight(w, fmt):
    k, n = w.shape
    w = f64(bf(w)).reshape(k // 32, 32, n)
    amax = np.abs(w).max(1)
    if fmt == "e4m3":
        byte = np.frexp(amax)[1] - 1 + 127 - 7
    else:
        mant, ex = np.frexp(amax / 6.0)
        byte = np.where(mant > 0.5, ex, ex - 1) + 127
    byte = np.clip(np.where(amax > 0, byte, 1), 1, 254)
    scaled = (w * np.exp2(127.0 - byte)[:, None, :]).reshape(k, n).astype(np.float32)
    by_word = np.ascontiguousarray(scaled.reshape(k // 512, 128, 4, n).transpose(0, 1, 3, 2))
    if fmt == "e4m3":
        words = by_word.astype(ml_dtypes.float8_e4m3fn).view(np.uint8)
    else:
        c = by_word.astype(ml_dtypes.float4_e2m1fn).view(np.uint8) & 0xF
        words = c[..., 0::2] | (c[..., 1::2] << 4)
    return np.ascontiguousarray(words), np.ascontiguousarray(byte.astype(np.uint8).reshape(k // 512, 16, n))


def unpack_weight(words, scales, fmt):
    g, p, n, _ = words.shape
    if fmt == "e4m3":
        vals = np.ascontiguousarray(words).view(ml_dtypes.float8_e4m3fn).astype(np.float64)
    else:
        nib = np.empty((g, p, n, 4), np.uint8)
        nib[..., 0::2] = words & 0xF
        nib[..., 1::2] = words >> 4
        vals = E2M1[nib]
    vals = vals * np.repeat(np.exp2(scales.astype(np.float64) - 127.0), 8, axis=1)[..., None]
    return vals.transpose(0, 1, 3, 2).reshape(g * 512, n)
def pack4(w):
    words, scales = pack_weight(w, "e2m1")
    return words.reshape(words.shape[0], 128, -1), scales


def unpack4(words, scales):
    return unpack_weight(words.reshape(words.shape[0], 128, -1, 2), scales, "e2m1")


M, K, F = 1024, 1024, 512


def sigmoid(v):
    return 1.0 / (1.0 + np.exp(-v))


def setup_inputs():
    s, t = mx_kscale(K), mx_kscale(F)
    tt = np.concatenate([t, t])
    lift = np.random.standard_normal((K, 4 * F)) / np.sqrt(K) / s[:, None]
    modes = 2.0 * np.random.standard_normal((2 * F, K)) / np.sqrt(2 * F) / tt[:, None]
    lift_words, lift_scales = pack4(lift)
    modes_words, modes_scales = pack_weight(modes, "e4m3")
    bias = 0.3 * np.random.standard_normal(4 * F)
    bias[3 * F:] += 1.0
    return {"x": bf(np.random.standard_normal((M, K)) * s),
            "lift_words": lift_words,
            "lift_scales": lift_scales,
            "bias": bf(bias),
            "omega": bf(np.random.uniform(-0.9, 0.9, F)),
            "nu": bf(np.random.uniform(0.3, 0.6, F)),
            "amp": bf((1.0 + 0.1 * np.random.standard_normal(F)) * t),
            "modes_words": modes_words,
            "modes_scales": modes_scales,
            "unit": bf((1.0 + 0.1 * np.random.standard_normal(K)) / s),
            "offset": bf(0.3 * np.random.standard_normal(K))}


def reference(x, lift_words, lift_scales, bias, omega, nu, amp, modes_words, modes_scales, unit, offset):
    x = f64(x)
    h = (mxq(x, 1, "e4m3") @ unpack4(lift_words, lift_scales)) + f64(bias)
    re = np.tanh(h[:, :F])
    im = np.tanh(h[:, F:2 * F])
    theta = f64(omega) + f64(nu) * np.tanh(h[:, 2 * F:3 * F])
    rho = f64(amp) * sigmoid(h[:, 3 * F:])
    c, d = np.cos(theta), np.sin(theta)
    z = np.concatenate([rho * (re * c - im * d), rho * (re * d + im * c)], axis=1)
    y = mxq(z, 1, "e4m3") @ unpack_weight(modes_words, modes_scales, "e4m3")
    return x * f64(unit) + y + f64(offset)

@@ -1,0 +1,461 @@
+import math
+from contextlib import ExitStack
+
+import concourse.mybir as mybir
+from concourse.masks import make_identity
+
+F32 = mybir.dt.float32
+BF16 = mybir.dt.bfloat16
+I32 = mybir.dt.int32
+U32 = mybir.dt.uint32
+U8 = mybir.dt.uint8
+E4M3X4 = mybir.dt.float8_e4m3fn_x4
+E2M1X4 = mybir.dt.float4_e2m1fn_x4
+ACT = mybir.ActivationFunctionType
+ALU = mybir.AluOpType
+
+P = 128
+ROWS = 1024
+CH = 1024
+MODES = 512
+LIFT = 4 * MODES
+S = 512
+FLOPS = 2 * ROWS * CH * LIFT + 2 * ROWS * 2 * MODES * CH
+
+RE, IM, FREQ, DAMP = 0, 1, 2, 3
+
+
+def tile_koopman_step_readout_f7_kernel(
+    tc, x, lift_words, lift_scales, bias, omega, nu, amp, modes_words, modes_scales, unit, offset, out
+):
+    nc = tc.nc
+    with ExitStack() as ctx:
+        keep = ctx.enter_context(tc.tile_pool(name="keep", bufs=1))
+        work = ctx.enter_context(tc.tile_pool(name="work", bufs=3))
+        psum = ctx.enter_context(tc.psum_pool(name="psum", bufs=1))
+        ctx.enter_context(tc.manual_schedule())
+
+        bias_c = keep.tile([P, 4, 4], BF16, name="bias_c")
+        omega_c = keep.tile([P, 4], BF16, name="omega_c")
+        nu_c = keep.tile([P, 4], BF16, name="nu_c")
+        amp_c = keep.tile([P, 4], BF16, name="amp_c")
+        unit_c = keep.tile([P, 2, 4], BF16, name="unit_c")
+        off_c = keep.tile([P, 8], F32, name="off_c")
+        off_r = keep.tile([P, CH], BF16, name="off_r", align_bytes=64)
+        ones = keep.tile([P, P], BF16, name="ones", align_bytes=64)
+        warm = keep.tile([P, 1], F32, name="warm")
+        ident = keep.tile([P, P], F32, name="ident", align_bytes=64)
+        diag = keep.tile([P, 8, P], BF16, name="diag", align_bytes=64)
+
+        w_raw = keep.tile([P, 2, 2 * LIFT], U8, name="w_raw", align_bytes=64)
+        w_perm = keep.tile([P, 4, 2, 2 * LIFT // 4], U8, name="w_perm", align_bytes=64)
+        ws_raw = keep.tile([P, 2, LIFT], U8, name="ws_raw", align_bytes=64)
+        ws_perm = keep.tile([P, 4, 2, LIFT // 4], U8, name="ws_perm", align_bytes=64)
+        v_codes = keep.tile([P, 2, CH * 4], U8, name="v_codes", align_bytes=64)
+        v_scales = keep.tile([P, 2, CH], U8, name="v_scales", align_bytes=64)
+
+        nc.vector.memset(warm[:], 0.0)
+        nc.vector.memset(ws_raw[:].rearrange("p g n -> p (g n)").bitcast(I32), 0)
+        make_identity(nc, ident[:])
+
+        ws_src = lift_scales.bitcast(I32).rearrange("g (a r) n -> r a g n", r=4)
+        for r in range(4):
+            nc.scalar.dma_start(out=ws_raw[r:P:32, :, :].bitcast(I32), in_=ws_src[r])
+        nc.scalar.dma_start(out=bias_c[:], in_=bias.rearrange("(a p t) -> p a t", a=4, t=4))
+        nc.scalar.dma_start(out=omega_c[:], in_=omega.rearrange("(p t) -> p t", t=4))
+        nc.scalar.dma_start(out=nu_c[:], in_=nu.rearrange("(p t) -> p t", t=4))
+        nc.scalar.dma_start(out=amp_c[:], in_=amp.rearrange("(p t) -> p t", t=4))
+        nc.scalar.activation(warm[:], warm[:], ACT.Silu)
+
+        x_rows = [keep.tile([P, CH], BF16, name="x%d" % row, align_bytes=64) for row in range(8)]
+        for row in range(4):
+            nc.sync.dma_start(out=x_rows[row][:], in_=x[row * P : (row + 1) * P, :])
+        for g in range(2):
+            nc.sync.dma_start(out=w_raw[:, g, :].bitcast(I32), in_=lift_words[g].bitcast(I32))
+        for row in range(4, 8):
+            nc.sync.dma_start(out=x_rows[row][:], in_=x[row * P : (row + 1) * P, :])
+
+        nc.gpsimd.memset(v_scales[:].rearrange("p g n -> p (g n)").bitcast(I32), 0)
+        nc.gpsimd.memset(ones[:], 1.0)
+        nc.gpsimd.memset(off_r[:], 0.0)
+        half_b = keep.tile([P, 4], F32, name="half_b")
+        half_amp = keep.tile([P, 4], F32, name="half_amp")
+        nu_f = keep.tile([P, 4], F32, name="nu_f")
+        omega_f = keep.tile([P, 4], F32, name="omega_f")
+        nsign = keep.tile([P, 4], F32, name="nsign")
+        cos_s = keep.tile([P, 4], F32, name="cos_s")
+        cos_b = keep.tile([P, 4], F32, name="cos_b")
+        nc.gpsimd.tensor_scalar(half_b[:], bias_c[:, DAMP, :], 0.5, None, ALU.mult)
+        nc.gpsimd.tensor_copy(out=omega_f[:], in_=omega_c[:])
+        nc.gpsimd.tensor_copy(out=nu_f[:], in_=nu_c[:])
+        nc.gpsimd.tensor_scalar(nsign[:], omega_f[:], 0.0, -2.0, ALU.is_ge, ALU.mult)
+        nc.gpsimd.tensor_scalar(nsign[:], nsign[:], 1.0, None, ALU.add)
+        nc.gpsimd.tensor_tensor(cos_s[:], nsign[:], nu_f[:], ALU.mult)
+        nc.gpsimd.tensor_tensor(cos_b[:], nsign[:], omega_f[:], ALU.mult)
+        nc.gpsimd.tensor_scalar(cos_b[:], cos_b[:], math.pi / 2, None, ALU.add)
+        nc.gpsimd.tensor_scalar(half_amp[:], amp_c[:], 0.5, None, ALU.mult)
+
+        vs_src = modes_scales.bitcast(I32).rearrange("g (a r) n -> r a g n", r=4)
+        for r in range(4):
+            nc.sync.dma_start(out=v_scales[r:P:32, :, :].bitcast(I32), in_=vs_src[r])
+        nc.sync.dma_start(out=unit_c[:], in_=unit.rearrange("(g p t) -> p g t", g=2, t=4))
+        nc.sync.dma_start(out=off_r[0:1, :], in_=offset.unsqueeze(0))
+        for g in range(2):
+            nc.sync.dma_start(out=v_codes[:, g, :].bitcast(I32), in_=modes_words[g].rearrange("p n t -> p (n t)").bitcast(I32))
+        for g in range(2):
+            for t in range(4):
+                nc.gpsimd.tensor_scalar(diag[:, 4 * g + t, :], ident[:], unit_c[:, g, t : t + 1], None, ALU.mult)
+
+        xg = [keep.tile([P, 2, S, 4], BF16, name="xg%d" % c, align_bytes=64) for c in range(2)]
+        xc = [keep.tile([P, 2, S], U32, name="xc%d" % c, align_bytes=64) for c in range(2)]
+        xs = [keep.tile([P, 2, S], U8, name="xs%d" % c, align_bytes=64) for c in range(2)]
+        zg = [keep.tile([P, 2, S, 4], BF16, name="zg%d" % c, align_bytes=64) for c in range(2)]
+        zc = [keep.tile([P, 2, S], U32, name="zc%d" % c, align_bytes=64) for c in range(2)]
+        zs = [keep.tile([P, 2, S], U8, name="zs%d" % c, align_bytes=64) for c in range(2)]
+        y_t = keep.tile([P, 8, S], F32, name="y_t", align_bytes=64)
+        res = [keep.tile([P, CH], F32, name="res%d" % row, align_bytes=64) for row in range(8)]
+        live = {}
+
+        def x_transpose(row):
+            words = x_rows[row][:].bitcast(F32)
+            bank = psum.tile([P, 4, P], F32, name="o", bufs=2)
+            for g in range(2):
+                for u in range(2):
+                    nc.tensor.transpose(bank[:, 2 * g + u, :], words[:, 256 * g + u : 256 * (g + 1) : 2], ident[:])
+            live["xt", row] = bank
+
+        def x_copy(row):
+            c, r = divmod(row, 4)
+            dst = xg[c][:].rearrange("p g s j -> p (g s j)").bitcast(F32).rearrange("p (g s u) -> p g s u", g=2, u=2)
+            src = live["xt", row][:].rearrange("p (g u) s -> p g s u", u=2)
+            nc.scalar.copy(out=dst[:, :, r * P : (r + 1) * P, :], in_=src)
+
+        def x_copy_v(row):
+            c, r = divmod(row, 4)
+            dst = xg[c][:].rearrange("p g s j -> p (g s j)").bitcast(F32).rearrange("p (g s u) -> p g s u", g=2, u=2)
+            src = live["xt", row][:].rearrange("p (g u) s -> p g s u", u=2)
+            nc.vector.tensor_copy(out=dst[:, :, r * P : (r + 1) * P, :], in_=src)
+
+        def x_quant(c, g):
+            nc.vector.quantize_mx(
+                out=xc[c][:, g, :].bitcast(E4M3X4),
+                scales=xs[c][:, g, :],
+                in_=xg[c][:, g, :, :].rearrange("p s j -> p (s j)"),
+            )
+
+        def w_permute(t, groups):
+            src = w_raw[:].rearrange("p g (n t b) -> p t g n b", t=4, b=2)
+            dst = w_perm[:].rearrange("p t g (n b) -> p t g n b", b=2)
+            nc.vector.tensor_copy(out=dst[:, t, groups], in_=src[:, t, groups])
+
+        def ws_permute(t):
+            src = ws_raw[:].rearrange("p g (n t) -> p t g n", t=4)
+            nc.vector.tensor_copy(out=ws_perm[:, t], in_=src[:, t])
+
+        def lift(u, part):
+            c, t = divmod(u, 4)
+            bank = psum.tile([P, S], F32, name="h%d" % part)
+            for g in range(2):
+                nc.tensor.matmul_mx(
+                    out=bank[:],
+                    lhsT=w_perm[:, t, g, 2 * P * part : 2 * P * (part + 1)].bitcast(E2M1X4),
+                    lhsT_scale=ws_perm[:, t, g, P * part : P * (part + 1)],
+                    rhs=xc[c][:, g, :].bitcast(E4M3X4),
+                    rhs_scale=xs[c][:, g, :],
+                    start=(g == 0),
+                    stop=(g == 1),
+                )
+            live["h", u, part] = bank
+
+        def lift_all(u):
+            for part in (FREQ, DAMP, RE, IM):
+                lift(u, part)
+
+        def act(u):
+            t = u % 4
+            tf = work.tile([P, S], F32, name="tf", bufs=2)
+            td = work.tile([P, S], F32, name="td")
+            trig = work.tile([P, 2, S], F32, name="trig")
+            tre = work.tile([P, S], F32, name="tre")
+            tim = work.tile([P, S], F32, name="tim")
+            nc.scalar.activation(tf[:], live["h", u, FREQ][:], ACT.Tanh, bias=bias_c[:, FREQ, t : t + 1])
+            nc.scalar.activation(td[:], live["h", u, DAMP][:], ACT.Tanh, bias=half_b[:, t : t + 1], scale=0.5)
+            nc.scalar.activation(trig[:, 0, :], tf[:], ACT.Sin, bias=cos_b[:, t : t + 1], scale=cos_s[:, t : t + 1])
+            nc.scalar.activation(trig[:, 1, :], tf[:], ACT.Sin, bias=omega_f[:, t : t + 1], scale=nu_f[:, t : t + 1])
+            nc.scalar.activation(tre[:], live["h", u, RE][:], ACT.Tanh, bias=bias_c[:, RE, t : t + 1])
+            nc.scalar.activation(tim[:], live["h", u, IM][:], ACT.Tanh, bias=bias_c[:, IM, t : t + 1])
+            live["a", u] = (td, trig, tre, tim)
+
+        def v1(u):
+            td, trig, tre, tim = live["a", u]
+            rot = work.tile([P, 2, S], F32, name="rot", bufs=2)
+            nc.vector.scalar_tensor_tensor(
+                out=rot[:], in0=td[:].unsqueeze(1).to_broadcast([P, 2, S]), scalar=1.0, in1=trig[:], op0=ALU.add, op1=ALU.mult
+            )
+            live["rot", u] = rot
+
+        def v23(u, which):
+            t = u % 4
+            if t == 0:
+                live["p", which] = work.tile([P, 4, 2, S], F32, name="p%d" % which, bufs=1)
+            src = live["a", u][2 + which]
+            nc.vector.scalar_tensor_tensor(
+                out=live["p", which][:, t, :, :],
+                in0=src[:].unsqueeze(1).to_broadcast([P, 2, S]),
+                scalar=half_amp[:, t : t + 1],
+                in1=live["rot", u][:],
+                op0=ALU.mult,
+                op1=ALU.mult,
+            )
+
+        def v2(u):
+            v23(u, 0)
+
+        def v3(u):
+            v23(u, 1)
+
+        def z_step(c, part, lo, hi):
+            a = live["p", 0][:, :, part, lo:hi].rearrange("p t (c i) -> p c t i", i=4)
+            b = live["p", 1][:, :, 1 - part, lo:hi].rearrange("p t (c i) -> p c t i", i=4)
+            dst = zg[c][:, part, lo:hi, :].rearrange("p (c i) t -> p c t i", i=4)
+            nc.vector.tensor_tensor(dst, a, b, ALU.subtract if part == 0 else ALU.add)
+
+        def z_quant(c, part, lo, hi):
+            nc.vector.quantize_mx(
+                out=zc[c][:, part, lo:hi].bitcast(E4M3X4),
+                scales=zs[c][:, part, lo:hi],
+                in_=zg[c][:, part, lo:hi, :].rearrange("p s j -> p (s j)"),
+            )
+
+        def add_x(bank, row, g, start, stop):
+            c, r = divmod(row, 4)
+            cols = bank[:].rearrange("p (m t) -> p t m", t=4)
+            for t in range(4):
+                nc.tensor.matmul(
+                    cols[:, t, :],
+                    lhsT=xg[c][:, g, r * P : (r + 1) * P, t],
+                    rhs=diag[:, 4 * g + t, :],
+                    start=(start and t == 0),
+                    stop=(stop and t == 3),
+                )
+
+        def yt_mm(j):
+            bank = psum.tile([P, S], F32, name="y", bufs=2)
+            for g in range(2):
+                nc.tensor.matmul_mx(
+                    out=bank[:],
+                    lhsT=v_codes[:, g, 4 * P * j : 4 * P * (j + 1)].bitcast(E4M3X4),
+                    lhsT_scale=v_scales[:, g, P * j : P * (j + 1)],
+                    rhs=zc[0][:, g, :].bitcast(E4M3X4),
+                    rhs_scale=zs[0][:, g, :],
+                    start=(g == 0),
+                    stop=(g == 1),
+                )
+            live["yt", j] = bank
+
+        def yt_copy(j):
+            nc.scalar.activation(y_t[:, j, :], live["yt", j][:], ACT.Identity, bias=off_c[:, j : j + 1])
+
+        def o_mm(row, h):
+            bank = psum.tile([P, S], F32, name="h%d" % row)
+            add_x(bank, row, h, True, False)
+            for k in range(4):
+                nc.tensor.matmul(
+                    bank[:, k * P : (k + 1) * P],
+                    lhsT=y_t[:, 4 * h + k, row * P : (row + 1) * P],
+                    rhs=ident[:],
+                    is_transpose=True,
+                    start=False,
+                    stop=(k == 3),
+                )
+            live["o", row, h] = bank
+
+        def offset_mm():
+            bank = psum.tile([P, S], F32, name="o", bufs=2)
+            for j in range(8):
+                nc.tensor.matmul(bank[:, j : j + 1], lhsT=off_r[:, j * P : (j + 1) * P], rhs=ones[:, 0:1], start=True, stop=True)
+            live["off"] = bank
+
+        def offset_copy():
+            nc.scalar.copy(out=off_c[:], in_=live["off"][:, 0:8])
+
+        def o_copy(row, h):
+            nc.scalar.copy(out=res[row][:, h * S : (h + 1) * S], in_=live["o", row, h][:])
+
+        def r_mm(row, h):
+            bank = psum.tile([P, S], F32, name="o", bufs=2)
+            nc.tensor.matmul(bank[:], lhsT=ones[:], rhs=off_r[:, h * S : (h + 1) * S], start=True, stop=False)
+            add_x(bank, row, h, False, True)
+            live["o", row, h] = bank
+
+        def y_mm(row, h):
+            c, r = divmod(row, 4)
+            bank = psum.tile([P, S], F32, name="y", bufs=2)
+            for g in range(2):
+                nc.tensor.matmul_mx(
+                    out=bank[:],
+                    lhsT=zc[c][:, g, r * P : (r + 1) * P].bitcast(E4M3X4),
+                    lhsT_scale=zs[c][:, g, r * P : (r + 1) * P],
+                    rhs=v_codes[:, g, 4 * h * S : 4 * (h + 1) * S].bitcast(E4M3X4),
+                    rhs_scale=v_scales[:, g, h * S : (h + 1) * S],
+                    start=(g == 0),
+                    stop=(g == 1),
+                )
+            live["y", row, h] = bank
+
+        def y_add(row, h):
+            half = res[row][:, h * S : (h + 1) * S]
+            nc.vector.tensor_tensor(half, live["y", row, h][:], half, ALU.add)
+
+        def store(row):
+            nc.sync.dma_start(out=out[row * P : (row + 1) * P, :], in_=res[row][:])
+
+        def store_half(row, h):
+            nc.sync.dma_start(out=out[row * P : (row + 1) * P, h * S : (h + 1) * S], in_=res[row][:, h * S : (h + 1) * S])
+
+        for t in range(4):
+            ws_permute(t)
+        for row in range(2):
+            x_transpose(row)
+            x_copy(row)
+        x_transpose(2)
+        x_copy_v(2)
+        w_permute(0, slice(0, 1))
+        x_transpose(3)
+        x_copy(3)
+        x_quant(0, 0)
+        x_quant(0, 1)
+        w_permute(0, slice(1, 2))
+        lift_all(0)
+        w_permute(1, slice(0, 2))
+        act(0)
+        x_transpose(4)
+        x_transpose(5)
+        lift_all(1)
+        w_permute(2, slice(0, 2))
+        x_copy(4)
+        w_permute(3, slice(0, 2))
+        v1(0)
+        v2(0)
+        act(1)
+        x_copy(5)
+        x_transpose(6)
+        lift_all(2)
+        x_transpose(7)
+        v3(0)
+        v1(1)
+        v2(1)
+        x_copy(6)
+        act(2)
+        lift_all(3)
+        v3(1)
+        x_copy_v(7)
+        v1(2)
+        x_quant(1, 0)
+        v2(2)
+        act(3)
+        x_quant(1, 1)
+        v3(2)
+        offset_mm()
+        lift_all(4)
+        v1(3)
+        v2(3)
+        offset_copy()
+        act(4)
+        r_mm(4, 0)
+        r_mm(4, 1)
+        lift_all(5)
+        v3(3)
+        act(5)
+        v1(4)
+        o_copy(4, 0)
+        o_copy(4, 1)
+        lift_all(6)
+        r_mm(5, 0)
+        r_mm(5, 1)
+        z_step(0, 0, 0, S)
+        z_step(0, 1, 0, S)
+        z_quant(0, 0, 0, S)
+        v2(4)
+        z_quant(0, 1, 0, S)
+        v1(5)
+        o_copy(5, 0)
+        o_copy(5, 1)
+        r_mm(6, 0)
+        r_mm(6, 1)
+        v3(4)
+        v2(5)
+        act(6)
+        lift_all(7)
+        v1(6)
+        v3(5)
+        v2(6)
+        yt_mm(0)
+        yt_mm(1)
+        act(7)
+        v1(7)
+        v3(6)
+        v2(7)
+        v3(7)
+
+        for j in range(8):
+            yt_copy(j)
+            if j < 6:
+                yt_mm(j + 2)
+            if j == 4:
+                o_mm(0, 0)
+            if j == 5:
+                o_mm(1, 0)
+        o_copy(6, 0)
+        o_copy(6, 1)
+        o_mm(2, 0)
+        r_mm(7, 0)
+        r_mm(7, 1)
+        o_copy(0, 0)
+        o_mm(3, 0)
+        o_copy(1, 0)
+        o_copy(7, 0)
+        o_copy(7, 1)
+        z_step(1, 0, 0, 256)
+        z_step(1, 1, 0, 256)
+        z_quant(1, 0, 0, 256)
+        z_step(1, 0, 256, 512)
+        z_quant(1, 1, 0, 256)
+        z_step(1, 1, 256, 512)
+        z_quant(1, 0, 256, 512)
+        z_quant(1, 1, 256, 512)
+        o_copy(2, 0)
+        o_mm(0, 1)
+        o_copy(3, 0)
+        o_copy(0, 1)
+        store(0)
+        y_mm(4, 0)
+        y_mm(4, 1)
+        o_mm(1, 1)
+        o_copy(1, 1)
+        store(1)
+        y_add(4, 0)
+        y_mm(5, 0)
+        y_add(4, 1)
+        store(4)
+        y_mm(5, 1)
+        y_add(5, 0)
+        y_mm(6, 0)
+        y_add(5, 1)
+        store(5)
+        y_mm(6, 1)
+        o_mm(2, 1)
+        o_copy(2, 1)
+        store(2)
+        y_add(6, 0)
+        y_mm(7, 0)
+        y_add(6, 1)
+        store(6)
+        y_mm(7, 1)
+        o_mm(3, 1)
+        o_copy(3, 1)
+        store(3)
+        y_add(7, 0)
+        store_half(7, 0)
+        y_add(7, 1)
+        store_half(7, 1)

@@ -42,6 +42,8 @@ def tile_koopman_step_readout_f7_kernel(
         unit_c = keep.tile([P, 2, 4], BF16, name="unit_c")
         off_c = keep.tile([P, 8], F32, name="off_c")
         off_r = keep.tile([P, CH], BF16, name="off_r", align_bytes=64)
+        off_p = keep.tile([P, 2, 4, P], BF16, name="off_p", align_bytes=64)
+        ident_p = keep.tile([P, 4, 32], F32, name="ident_p", align_bytes=64)
         ones = keep.tile([P, P], BF16, name="ones", align_bytes=64)
         warm = keep.tile([P, 1], F32, name="warm")
         ident = keep.tile([P, P], F32, name="ident", align_bytes=64)
@@ -54,30 +56,42 @@ def tile_koopman_step_readout_f7_kernel(
         v_codes = keep.tile([P, 2, CH * 4], U8, name="v_codes", align_bytes=64)
         v_scales = keep.tile([P, 2, CH], U8, name="v_scales", align_bytes=64)
 
-        nc.vector.memset(warm[:], 0.0)
+        x_rows = []
+        x_tiles = [keep.tile([P, n, CH], BF16, name="x%d" % k, align_bytes=64) for k, n in enumerate((1, 1, 2, 2, 2))]
+        for tile in x_tiles:
+            x_rows += [tile[:, i, :] for i in range(tile.shape[1])]
+
+        def load_x(k):
+            n = x_tiles[k].shape[1]
+            row = (0, 1, 2, 4, 6)[k]
+            src = x[row * P : (row + n) * P, :].rearrange("(i p) c -> p i c", p=P)
+            nc.sync.dma_start(out=x_tiles[k][:], in_=src)
+
         nc.vector.memset(ws_raw[:].rearrange("p g n -> p (g n)").bitcast(I32), 0)
+        nc.vector.memset(warm[:], 0.0)
         make_identity(nc, ident[:])
 
+        nc.scalar.dma_start(out=unit_c[:], in_=unit.rearrange("(g p t) -> p g t", g=2, t=4))
+        load_x(0)
+        load_x(1)
+        load_x(2)
         ws_src = lift_scales.bitcast(I32).rearrange("g (a r) n -> r a g n", r=4)
         for r in range(4):
             nc.scalar.dma_start(out=ws_raw[r:P:32, :, :].bitcast(I32), in_=ws_src[r])
-        nc.scalar.dma_start(out=bias_c[:], in_=bias.rearrange("(a p t) -> p a t", a=4, t=4))
-        nc.scalar.dma_start(out=omega_c[:], in_=omega.rearrange("(p t) -> p t", t=4))
-        nc.scalar.dma_start(out=nu_c[:], in_=nu.rearrange("(p t) -> p t", t=4))
-        nc.scalar.dma_start(out=amp_c[:], in_=amp.rearrange("(p t) -> p t", t=4))
         nc.scalar.activation(warm[:], warm[:], ACT.Silu)
-
-        x_rows = [keep.tile([P, CH], BF16, name="x%d" % row, align_bytes=64) for row in range(8)]
-        for row in range(4):
-            nc.sync.dma_start(out=x_rows[row][:], in_=x[row * P : (row + 1) * P, :])
         for g in range(2):
             nc.sync.dma_start(out=w_raw[:, g, :].bitcast(I32), in_=lift_words[g].bitcast(I32))
-        for row in range(4, 8):
-            nc.sync.dma_start(out=x_rows[row][:], in_=x[row * P : (row + 1) * P, :])
+        nc.gpsimd.dma_start(out=bias_c[:], in_=bias.rearrange("(a p t) -> p a t", a=4, t=4))
+        nc.gpsimd.dma_start(out=omega_c[:], in_=omega.rearrange("(p t) -> p t", t=4))
+        nc.gpsimd.dma_start(out=nu_c[:], in_=nu.rearrange("(p t) -> p t", t=4))
+        nc.gpsimd.dma_start(out=amp_c[:], in_=amp.rearrange("(p t) -> p t", t=4))
+        load_x(3)
+        load_x(4)
+        nc.vector.tensor_copy(out=ident_p[:], in_=ident[:].rearrange("p (q t) -> p t q", t=4))
+        for g in range(2):
+            for t in range(4):
+                nc.vector.tensor_scalar(diag[:, 4 * g + t, :], ident[:], unit_c[:, g, t : t + 1], None, ALU.mult)
 
-        nc.gpsimd.memset(v_scales[:].rearrange("p g n -> p (g n)").bitcast(I32), 0)
-        nc.gpsimd.memset(ones[:], 1.0)
-        nc.gpsimd.memset(off_r[:], 0.0)
         half_b = keep.tile([P, 4], F32, name="half_b")
         half_amp = keep.tile([P, 4], F32, name="half_amp")
         nu_f = keep.tile([P, 4], F32, name="nu_f")
@@ -95,16 +109,20 @@ def tile_koopman_step_readout_f7_kernel(
         nc.gpsimd.tensor_scalar(cos_b[:], cos_b[:], math.pi / 2, None, ALU.add)
         nc.gpsimd.tensor_scalar(half_amp[:], amp_c[:], 0.5, None, ALU.mult)
 
+        nc.gpsimd.memset(v_scales[:].rearrange("p g n -> p (g n)").bitcast(I32), 0)
+        nc.gpsimd.memset(ones[:], 1.0)
+        nc.gpsimd.memset(off_r[:], 0.0)
+        nc.gpsimd.memset(off_p[:], 0.0)
         vs_src = modes_scales.bitcast(I32).rearrange("g (a r) n -> r a g n", r=4)
         for r in range(4):
             nc.sync.dma_start(out=v_scales[r:P:32, :, :].bitcast(I32), in_=vs_src[r])
-        nc.sync.dma_start(out=unit_c[:], in_=unit.rearrange("(g p t) -> p g t", g=2, t=4))
         nc.sync.dma_start(out=off_r[0:1, :], in_=offset.unsqueeze(0))
         for g in range(2):
             nc.sync.dma_start(out=v_codes[:, g, :].bitcast(I32), in_=modes_words[g].rearrange("p n t -> p (n t)").bitcast(I32))
-        for g in range(2):
-            for t in range(4):
-                nc.gpsimd.tensor_scalar(diag[:, 4 * g + t, :], ident[:], unit_c[:, g, t : t + 1], None, ALU.mult)
+
+        nc.gpsimd.tensor_scalar(
+            off_p[0:1], off_r[0:1, :].rearrange("o (g m t) -> o g t m", g=2, t=4), 1.0, 0.0, ALU.mult, ALU.add
+        )
 
         xg = [keep.tile([P, 2, S, 4], BF16, name="xg%d" % c, align_bytes=64) for c in range(2)]
         xc = [keep.tile([P, 2, S], U32, name="xc%d" % c, align_bytes=64) for c in range(2)]
@@ -117,7 +135,7 @@ def tile_koopman_step_readout_f7_kernel(
         live = {}
 
         def x_transpose(row):
-            words = x_rows[row][:].bitcast(F32)
+            words = x_rows[row].bitcast(F32)
             bank = psum.tile([P, 4, P], F32, name="o", bufs=2)
             for g in range(2):
                 for u in range(2):
@@ -229,7 +247,7 @@ def tile_koopman_step_readout_f7_kernel(
 
         def add_x(bank, row, g, start, stop):
             c, r = divmod(row, 4)
-            cols = bank[:].rearrange("p (m t) -> p t m", t=4)
+            cols = bank[:].rearrange("p (t m) -> p t m", t=4)
             for t in range(4):
                 nc.tensor.matmul(
                     cols[:, t, :],
@@ -261,9 +279,9 @@ def tile_koopman_step_readout_f7_kernel(
             add_x(bank, row, h, True, False)
             for k in range(4):
                 nc.tensor.matmul(
-                    bank[:, k * P : (k + 1) * P],
+                    bank[:].rearrange("p (t m) -> p t m", t=4)[:, :, 32 * k : 32 * (k + 1)],
                     lhsT=y_t[:, 4 * h + k, row * P : (row + 1) * P],
-                    rhs=ident[:],
+                    rhs=ident_p[:],
                     is_transpose=True,
                     start=False,
                     stop=(k == 3),
@@ -280,11 +298,14 @@ def tile_koopman_step_readout_f7_kernel(
             nc.scalar.copy(out=off_c[:], in_=live["off"][:, 0:8])
 
         def o_copy(row, h):
-            nc.scalar.copy(out=res[row][:, h * S : (h + 1) * S], in_=live["o", row, h][:])
+            nc.scalar.copy(
+                out=res[row][:, h * S : (h + 1) * S].rearrange("p (m t) -> p m t", t=4),
+                in_=live["o", row, h][:].rearrange("p (t m) -> p m t", t=4),
+            )
 
         def r_mm(row, h):
             bank = psum.tile([P, S], F32, name="o", bufs=2)
-            nc.tensor.matmul(bank[:], lhsT=ones[:], rhs=off_r[:, h * S : (h + 1) * S], start=True, stop=False)
+            nc.tensor.matmul(bank[:], lhsT=ones[:], rhs=off_p[:, h].rearrange("p t m -> p (t m)"), start=True, stop=False)
             add_x(bank, row, h, False, True)
             live["o", row, h] = bank
 
@@ -334,31 +355,31 @@ def tile_koopman_step_readout_f7_kernel(
         lift_all(1)
         w_permute(2, slice(0, 2))
         x_copy(4)
-        w_permute(3, slice(0, 2))
         v1(0)
+        w_permute(3, slice(0, 2))
         v2(0)
         act(1)
         x_copy(5)
         x_transpose(6)
         lift_all(2)
         x_transpose(7)
-        v3(0)
         v1(1)
+        v3(0)
         v2(1)
         x_copy(6)
         act(2)
         lift_all(3)
-        v3(1)
         x_copy_v(7)
         v1(2)
-        x_quant(1, 0)
+        v3(1)
         v2(2)
         act(3)
+        x_quant(1, 0)
         x_quant(1, 1)
-        v3(2)
         offset_mm()
         lift_all(4)
         v1(3)
+        v3(2)
         v2(3)
         offset_copy()
         act(4)
@@ -375,8 +396,8 @@ def tile_koopman_step_readout_f7_kernel(
         r_mm(5, 1)
         z_step(0, 0, 0, S)
         z_step(0, 1, 0, S)
-        z_quant(0, 0, 0, S)
         v2(4)
+        z_quant(0, 0, 0, S)
         z_quant(0, 1, 0, S)
         v1(5)
         o_copy(5, 0)

@@ -35,22 +35,24 @@ def tile_koopman_step_readout_f7_kernel(
         psum = ctx.enter_context(tc.psum_pool(name="psum", bufs=1))
         ctx.enter_context(tc.manual_schedule())
 
-        bias_c = keep.tile([P, 4, 4], BF16, name="bias_c")
-        omega_c = keep.tile([P, 4], BF16, name="omega_c")
-        nu_c = keep.tile([P, 4], BF16, name="nu_c")
-        amp_c = keep.tile([P, 4], BF16, name="amp_c")
-        unit_c = keep.tile([P, 2, 4], BF16, name="unit_c")
-        off_c = keep.tile([P, 8], F32, name="off_c")
-        off_r = keep.tile([P, CH], BF16, name="off_r", align_bytes=64)
+        vec_rows = keep.tile([P, MODES], BF16, name="vec_rows", align_bytes=64)
+        vec = keep.tile([P, 4, 16], F32, name="vec")
+        off_r = keep.tile([1, CH], BF16, name="off_r", align_bytes=64)
         off_p = keep.tile([P, 2, 4, P], BF16, name="off_p", align_bytes=64)
-        ident_p = keep.tile([P, 4, 32], F32, name="ident_p", align_bytes=64)
         ones = keep.tile([P, P], BF16, name="ones", align_bytes=64)
         warm = keep.tile([P, 1], F32, name="warm")
+        warm_b = keep.tile([P, S], BF16, name="warm_b", align_bytes=64)
         ident = keep.tile([P, P], F32, name="ident", align_bytes=64)
+        ident_b = keep.tile([P, P], BF16, name="ident_b", align_bytes=64)
         diag = keep.tile([P, 8, P], BF16, name="diag", align_bytes=64)
+        half_b = keep.tile([P, 4], F32, name="half_b")
+        half_amp = keep.tile([P, 4], F32, name="half_amp")
+        nsign = keep.tile([P, 4], F32, name="nsign")
+        cos_s = keep.tile([P, 4], F32, name="cos_s")
+        cos_b = keep.tile([P, 4], F32, name="cos_b")
 
-        w_raw = keep.tile([P, 2, 2 * LIFT], U8, name="w_raw", align_bytes=64)
-        w_perm = keep.tile([P, 4, 2, 2 * LIFT // 4], U8, name="w_perm", align_bytes=64)
+        w_raw = keep.tile([P, 2, 2, LIFT], U8, name="w_raw", align_bytes=64)
+        w_perm = keep.tile([P, 4, 2, 2, LIFT // 4], U8, name="w_perm", align_bytes=64)
         ws_raw = keep.tile([P, 2, LIFT], U8, name="ws_raw", align_bytes=64)
         ws_perm = keep.tile([P, 4, 2, LIFT // 4], U8, name="ws_perm", align_bytes=64)
         v_codes = keep.tile([P, 2, CH * 4], U8, name="v_codes", align_bytes=64)
@@ -67,62 +69,78 @@ def tile_koopman_step_readout_f7_kernel(
             src = x[row * P : (row + n) * P, :].rearrange("(i p) c -> p i c", p=P)
             nc.sync.dma_start(out=x_tiles[k][:], in_=src)
 
-        nc.vector.memset(ws_raw[:].rearrange("p g n -> p (g n)").bitcast(I32), 0)
-        nc.vector.memset(warm[:], 0.0)
-        make_identity(nc, ident[:])
+        def load_ws(r):
+            src = lift_scales.bitcast(I32).rearrange("g (a r) n -> r a g n", r=4)
+            nc.sync.dma_start(out=ws_raw[r:P:32, :, :].bitcast(I32), in_=src[r])
 
-        nc.scalar.dma_start(out=unit_c[:], in_=unit.rearrange("(g p t) -> p g t", g=2, t=4))
+        def load_w(half):
+            src = lift_words.bitcast(I32).rearrange("g p (h n) -> h p g n", h=2)
+            nc.sync.dma_start(out=w_raw[:, half].bitcast(I32), in_=src[half])
+
+        nc.vector.memset(warm[:], 0.0)
+        nc.vector.memset(warm_b[:].bitcast(I32), 0)
+        nc.vector.memset(vec_rows[:].bitcast(I32), 0)
+        nc.vector.memset(ws_raw[:].rearrange("p g n -> p (g n)").bitcast(I32), 0)
+        make_identity(nc, ident[:])
+        nc.scalar.dma_start(out=vec_rows[0:4, :], in_=bias.rearrange("(a n) -> a n", a=4))
+        nc.scalar.dma_start(out=vec_rows[4:5, :], in_=omega.unsqueeze(0))
+        nc.scalar.dma_start(out=vec_rows[5:6, :], in_=nu.unsqueeze(0))
+        nc.gpsimd.dma_start(out=vec_rows[6:7, :], in_=amp.unsqueeze(0))
+        nc.gpsimd.dma_start(out=vec_rows[7:9, :], in_=unit.rearrange("(a n) -> a n", a=2))
+        nc.scalar.activation(warm[:], warm[:], ACT.Silu)
         load_x(0)
         load_x(1)
         load_x(2)
-        ws_src = lift_scales.bitcast(I32).rearrange("g (a r) n -> r a g n", r=4)
         for r in range(4):
-            nc.scalar.dma_start(out=ws_raw[r:P:32, :, :].bitcast(I32), in_=ws_src[r])
-        nc.scalar.activation(warm[:], warm[:], ACT.Silu)
-        for g in range(2):
-            nc.sync.dma_start(out=w_raw[:, g, :].bitcast(I32), in_=lift_words[g].bitcast(I32))
-        nc.gpsimd.dma_start(out=bias_c[:], in_=bias.rearrange("(a p t) -> p a t", a=4, t=4))
-        nc.gpsimd.dma_start(out=omega_c[:], in_=omega.rearrange("(p t) -> p t", t=4))
-        nc.gpsimd.dma_start(out=nu_c[:], in_=nu.rearrange("(p t) -> p t", t=4))
-        nc.gpsimd.dma_start(out=amp_c[:], in_=amp.rearrange("(p t) -> p t", t=4))
+            load_ws(r)
+        load_w(1)
+        load_w(0)
         load_x(3)
         load_x(4)
-        nc.vector.tensor_copy(out=ident_p[:], in_=ident[:].rearrange("p (q t) -> p t q", t=4))
-        for g in range(2):
+        nc.vector.tensor_copy(out=ident_b[:], in_=ident[:])
+
+        def warm_up(n, late=False):
+            bank = psum.tile([P, S], F32, name="y", bufs=2)
+            rhs = xg[0][:, 0, 3 * P : S, :].rearrange("p s j -> p (s j)") if late else warm_b[:]
+            for i in range(n):
+                nc.tensor.matmul(bank[:], lhsT=warm_b[:, 0:P], rhs=rhs, start=True, stop=True)
+
+        def vec_transpose():
+            bank = psum.tile([P, 4, P], BF16, name="y", bufs=2)
             for t in range(4):
-                nc.vector.tensor_scalar(diag[:, 4 * g + t, :], ident[:], unit_c[:, g, t : t + 1], None, ALU.mult)
+                nc.tensor.transpose(bank[:, t, :], vec_rows[:, t : MODES : 4], ident_b[:])
+            live["vec"] = bank
 
-        half_b = keep.tile([P, 4], F32, name="half_b")
-        half_amp = keep.tile([P, 4], F32, name="half_amp")
-        nu_f = keep.tile([P, 4], F32, name="nu_f")
-        omega_f = keep.tile([P, 4], F32, name="omega_f")
-        nsign = keep.tile([P, 4], F32, name="nsign")
-        cos_s = keep.tile([P, 4], F32, name="cos_s")
-        cos_b = keep.tile([P, 4], F32, name="cos_b")
-        nc.gpsimd.tensor_scalar(half_b[:], bias_c[:, DAMP, :], 0.5, None, ALU.mult)
-        nc.gpsimd.tensor_copy(out=omega_f[:], in_=omega_c[:])
-        nc.gpsimd.tensor_copy(out=nu_f[:], in_=nu_c[:])
-        nc.gpsimd.tensor_scalar(nsign[:], omega_f[:], 0.0, -2.0, ALU.is_ge, ALU.mult)
-        nc.gpsimd.tensor_scalar(nsign[:], nsign[:], 1.0, None, ALU.add)
-        nc.gpsimd.tensor_tensor(cos_s[:], nsign[:], nu_f[:], ALU.mult)
-        nc.gpsimd.tensor_tensor(cos_b[:], nsign[:], omega_f[:], ALU.mult)
-        nc.gpsimd.tensor_scalar(cos_b[:], cos_b[:], math.pi / 2, None, ALU.add)
-        nc.gpsimd.tensor_scalar(half_amp[:], amp_c[:], 0.5, None, ALU.mult)
+        def vec_copy():
+            nc.vector.tensor_copy(out=vec[:], in_=live["vec"][:, :, 0:16])
 
-        nc.gpsimd.memset(v_scales[:].rearrange("p g n -> p (g n)").bitcast(I32), 0)
-        nc.gpsimd.memset(ones[:], 1.0)
-        nc.gpsimd.memset(off_r[:], 0.0)
-        nc.gpsimd.memset(off_p[:], 0.0)
-        vs_src = modes_scales.bitcast(I32).rearrange("g (a r) n -> r a g n", r=4)
-        for r in range(4):
-            nc.sync.dma_start(out=v_scales[r:P:32, :, :].bitcast(I32), in_=vs_src[r])
-        nc.sync.dma_start(out=off_r[0:1, :], in_=offset.unsqueeze(0))
-        for g in range(2):
-            nc.sync.dma_start(out=v_codes[:, g, :].bitcast(I32), in_=modes_words[g].rearrange("p n t -> p (n t)").bitcast(I32))
+        def vec_prepare():
+            nc.gpsimd.tensor_scalar(half_b[:], vec[:, :, DAMP], 0.5, None, ALU.mult)
+            nc.gpsimd.tensor_scalar(nsign[:], vec[:, :, 4], 0.0, -2.0, ALU.is_ge, ALU.mult)
+            nc.gpsimd.tensor_scalar(nsign[:], nsign[:], 1.0, None, ALU.add)
+            nc.gpsimd.tensor_tensor(cos_s[:], nsign[:], vec[:, :, 5], ALU.mult)
+            nc.gpsimd.tensor_tensor(cos_b[:], nsign[:], vec[:, :, 4], ALU.mult)
+            nc.gpsimd.tensor_scalar(cos_b[:], cos_b[:], math.pi / 2, None, ALU.add)
+            nc.gpsimd.tensor_scalar(half_amp[:], vec[:, :, 6], 0.5, None, ALU.mult)
 
-        nc.gpsimd.tensor_scalar(
-            off_p[0:1], off_r[0:1, :].rearrange("o (g m t) -> o g t m", g=2, t=4), 1.0, 0.0, ALU.mult, ALU.add
-        )
+        def diag_build():
+            for g in range(2):
+                for t in range(4):
+                    nc.scalar.activation(diag[:, 4 * g + t, :], ident[:], ACT.Copy, scale=vec[:, t, 7 + g : 8 + g])
+
+        def load_v():
+            nc.gpsimd.memset(v_scales[:].rearrange("p g n -> p (g n)").bitcast(I32), 0)
+            nc.gpsimd.memset(ones[:], 1.0)
+            nc.gpsimd.memset(off_p[:], 0.0)
+            src = modes_scales.bitcast(I32).rearrange("g (a r) n -> r a g n", r=4)
+            for r in range(4):
+                nc.sync.dma_start(out=v_scales[r:P:32, :, :].bitcast(I32), in_=src[r])
+            nc.sync.dma_start(out=off_r[0:1, :], in_=offset.unsqueeze(0))
+            for g in range(2):
+                nc.sync.dma_start(out=v_codes[:, g, :].bitcast(I32), in_=modes_words[g].rearrange("p n t -> p (n t)").bitcast(I32))
+            nc.gpsimd.tensor_scalar(
+                off_p[0:1], off_r[0:1, :].rearrange("o (g m t) -> o g t m", g=2, t=4), 1.0, 0.0, ALU.mult, ALU.add
+            )
 
         xg = [keep.tile([P, 2, S, 4], BF16, name="xg%d" % c, align_bytes=64) for c in range(2)]
         xc = [keep.tile([P, 2, S], U32, name="xc%d" % c, align_bytes=64) for c in range(2)]
@@ -130,13 +148,12 @@ def tile_koopman_step_readout_f7_kernel(
         zg = [keep.tile([P, 2, S, 4], BF16, name="zg%d" % c, align_bytes=64) for c in range(2)]
         zc = [keep.tile([P, 2, S], U32, name="zc%d" % c, align_bytes=64) for c in range(2)]
         zs = [keep.tile([P, 2, S], U8, name="zs%d" % c, align_bytes=64) for c in range(2)]
-        y_t = keep.tile([P, 8, S], F32, name="y_t", align_bytes=64)
         res = [keep.tile([P, CH], F32, name="res%d" % row, align_bytes=64) for row in range(8)]
         live = {}
 
         def x_transpose(row):
             words = x_rows[row].bitcast(F32)
-            bank = psum.tile([P, 4, P], F32, name="o", bufs=2)
+            bank = psum.tile([P, 4, P], F32, name="o" if row < 4 else "y", bufs=2)
             for g in range(2):
                 for u in range(2):
                     nc.tensor.transpose(bank[:, 2 * g + u, :], words[:, 256 * g + u : 256 * (g + 1) : 2], ident[:])
@@ -161,10 +178,10 @@ def tile_koopman_step_readout_f7_kernel(
                 in_=xg[c][:, g, :, :].rearrange("p s j -> p (s j)"),
             )
 
-        def w_permute(t, groups):
-            src = w_raw[:].rearrange("p g (n t b) -> p t g n b", t=4, b=2)
-            dst = w_perm[:].rearrange("p t g (n b) -> p t g n b", b=2)
-            nc.vector.tensor_copy(out=dst[:, t, groups], in_=src[:, t, groups])
+        def w_permute(t, half):
+            src = w_raw[:, half].rearrange("p g (n t b) -> p t g n b", t=4, b=2)
+            dst = w_perm[:, t, half].rearrange("p g (n b) -> p g n b", b=2)
+            nc.vector.tensor_copy(out=dst, in_=src[:, t])
 
         def ws_permute(t):
             src = ws_raw[:].rearrange("p g (n t) -> p t g n", t=4)
@@ -176,7 +193,7 @@ def tile_koopman_step_readout_f7_kernel(
             for g in range(2):
                 nc.tensor.matmul_mx(
                     out=bank[:],
-                    lhsT=w_perm[:, t, g, 2 * P * part : 2 * P * (part + 1)].bitcast(E2M1X4),
+                    lhsT=w_perm[:, t, part // 2, g, 2 * P * (part % 2) : 2 * P * (part % 2 + 1)].bitcast(E2M1X4),
                     lhsT_scale=ws_perm[:, t, g, P * part : P * (part + 1)],
                     rhs=xc[c][:, g, :].bitcast(E4M3X4),
                     rhs_scale=xs[c][:, g, :],
@@ -185,27 +202,28 @@ def tile_koopman_step_readout_f7_kernel(
                 )
             live["h", u, part] = bank
 
-        def lift_all(u):
-            for part in (FREQ, DAMP, RE, IM):
-                lift(u, part)
-
-        def act(u):
+        def act(u, kind):
             t = u % 4
-            tf = work.tile([P, S], F32, name="tf", bufs=2)
-            td = work.tile([P, S], F32, name="td")
-            trig = work.tile([P, 2, S], F32, name="trig")
-            tre = work.tile([P, S], F32, name="tre")
-            tim = work.tile([P, S], F32, name="tim")
-            nc.scalar.activation(tf[:], live["h", u, FREQ][:], ACT.Tanh, bias=bias_c[:, FREQ, t : t + 1])
-            nc.scalar.activation(td[:], live["h", u, DAMP][:], ACT.Tanh, bias=half_b[:, t : t + 1], scale=0.5)
-            nc.scalar.activation(trig[:, 0, :], tf[:], ACT.Sin, bias=cos_b[:, t : t + 1], scale=cos_s[:, t : t + 1])
-            nc.scalar.activation(trig[:, 1, :], tf[:], ACT.Sin, bias=omega_f[:, t : t + 1], scale=nu_f[:, t : t + 1])
-            nc.scalar.activation(tre[:], live["h", u, RE][:], ACT.Tanh, bias=bias_c[:, RE, t : t + 1])
-            nc.scalar.activation(tim[:], live["h", u, IM][:], ACT.Tanh, bias=bias_c[:, IM, t : t + 1])
-            live["a", u] = (td, trig, tre, tim)
+            if kind == "f":
+                live["f", u] = work.tile([P, S], F32, name="tf", bufs=2)
+                nc.scalar.activation(live["f", u][:], live["h", u, FREQ][:], ACT.Tanh, bias=vec[:, t, FREQ : FREQ + 1])
+            elif kind == "d":
+                live["d", u] = work.tile([P, S], F32, name="td")
+                nc.scalar.activation(live["d", u][:], live["h", u, DAMP][:], ACT.Tanh, bias=half_b[:, t : t + 1], scale=0.5)
+            elif kind == "c":
+                live["trig", u] = work.tile([P, 2, S], F32, name="trig")
+                nc.scalar.activation(live["trig", u][:, 0, :], live["f", u][:], ACT.Sin, bias=cos_b[:, t : t + 1], scale=cos_s[:, t : t + 1])
+            elif kind == "s":
+                nc.scalar.activation(live["trig", u][:, 1, :], live["f", u][:], ACT.Sin, bias=vec[:, t, 4:5], scale=vec[:, t, 5:6])
+            elif kind == "r":
+                live["r", u] = work.tile([P, S], F32, name="tre")
+                nc.scalar.activation(live["r", u][:], live["h", u, RE][:], ACT.Tanh, bias=vec[:, t, RE : RE + 1])
+            else:
+                live["i", u] = work.tile([P, S], F32, name="tim")
+                nc.scalar.activation(live["i", u][:], live["h", u, IM][:], ACT.Tanh, bias=vec[:, t, IM : IM + 1])
 
         def v1(u):
-            td, trig, tre, tim = live["a", u]
+            td, trig = live["d", u], live["trig", u]
             rot = work.tile([P, 2, S], F32, name="rot", bufs=2)
             nc.vector.scalar_tensor_tensor(
                 out=rot[:], in0=td[:].unsqueeze(1).to_broadcast([P, 2, S]), scalar=1.0, in1=trig[:], op0=ALU.add, op1=ALU.mult
@@ -214,11 +232,11 @@ def tile_koopman_step_readout_f7_kernel(
 
         def v23(u, which):
             t = u % 4
-            if t == 0:
-                live["p", which] = work.tile([P, 4, 2, S], F32, name="p%d" % which, bufs=1)
-            src = live["a", u][2 + which]
+            if ("p", u // 4, which) not in live:
+                live["p", u // 4, which] = work.tile([P, 4, 2, S], F32, name="p%d" % which, bufs=1)
+            src = live["ri"[which], u]
             nc.vector.scalar_tensor_tensor(
-                out=live["p", which][:, t, :, :],
+                out=live["p", u // 4, which][:, t, :, :],
                 in0=src[:].unsqueeze(1).to_broadcast([P, 2, S]),
                 scalar=half_amp[:, t : t + 1],
                 in1=live["rot", u][:],
@@ -233,8 +251,8 @@ def tile_koopman_step_readout_f7_kernel(
             v23(u, 1)
 
         def z_step(c, part, lo, hi):
-            a = live["p", 0][:, :, part, lo:hi].rearrange("p t (c i) -> p c t i", i=4)
-            b = live["p", 1][:, :, 1 - part, lo:hi].rearrange("p t (c i) -> p c t i", i=4)
+            a = live["p", c, 0][:, :, part, lo:hi].rearrange("p t (c i) -> p c t i", i=4)
+            b = live["p", c, 1][:, :, 1 - part, lo:hi].rearrange("p t (c i) -> p c t i", i=4)
             dst = zg[c][:, part, lo:hi, :].rearrange("p (c i) t -> p c t i", i=4)
             nc.vector.tensor_tensor(dst, a, b, ALU.subtract if part == 0 else ALU.add)
 
@@ -257,61 +275,18 @@ def tile_koopman_step_readout_f7_kernel(
                     stop=(stop and t == 3),
                 )
 
-        def yt_mm(j):
-            bank = psum.tile([P, S], F32, name="y", bufs=2)
-            for g in range(2):
-                nc.tensor.matmul_mx(
-                    out=bank[:],
-                    lhsT=v_codes[:, g, 4 * P * j : 4 * P * (j + 1)].bitcast(E4M3X4),
-                    lhsT_scale=v_scales[:, g, P * j : P * (j + 1)],
-                    rhs=zc[0][:, g, :].bitcast(E4M3X4),
-                    rhs_scale=zs[0][:, g, :],
-                    start=(g == 0),
-                    stop=(g == 1),
-                )
-            live["yt", j] = bank
-
-        def yt_copy(j):
-            nc.scalar.activation(y_t[:, j, :], live["yt", j][:], ACT.Identity, bias=off_c[:, j : j + 1])
-
-        def o_mm(row, h):
-            bank = psum.tile([P, S], F32, name="h%d" % row)
-            add_x(bank, row, h, True, False)
-            for k in range(4):
-                nc.tensor.matmul(
-                    bank[:].rearrange("p (t m) -> p t m", t=4)[:, :, 32 * k : 32 * (k + 1)],
-                    lhsT=y_t[:, 4 * h + k, row * P : (row + 1) * P],
-                    rhs=ident_p[:],
-                    is_transpose=True,
-                    start=False,
-                    stop=(k == 3),
-                )
-            live["o", row, h] = bank
-
-        def offset_mm():
-            bank = psum.tile([P, S], F32, name="o", bufs=2)
-            for j in range(8):
-                nc.tensor.matmul(bank[:, j : j + 1], lhsT=off_r[:, j * P : (j + 1) * P], rhs=ones[:, 0:1], start=True, stop=True)
-            live["off"] = bank
-
-        def offset_copy():
-            nc.scalar.copy(out=off_c[:], in_=live["off"][:, 0:8])
-
-        def o_copy(row, h):
-            nc.scalar.copy(
-                out=res[row][:, h * S : (h + 1) * S].rearrange("p (m t) -> p m t", t=4),
-                in_=live["o", row, h][:].rearrange("p (t m) -> p m t", t=4),
-            )
+        def offset_mm(bank, h):
+            nc.tensor.matmul(bank[:], lhsT=ones[:], rhs=off_p[:, h].rearrange("p t m -> p (t m)"), start=True, stop=False)
 
         def r_mm(row, h):
             bank = psum.tile([P, S], F32, name="o", bufs=2)
-            nc.tensor.matmul(bank[:], lhsT=ones[:], rhs=off_p[:, h].rearrange("p t m -> p (t m)"), start=True, stop=False)
+            offset_mm(bank, h)
             add_x(bank, row, h, False, True)
             live["o", row, h] = bank
 
         def y_mm(row, h):
             c, r = divmod(row, 4)
-            bank = psum.tile([P, S], F32, name="y", bufs=2)
+            bank = psum.tile([P, S], F32, name="o" if row in (5, 7) else "y", bufs=2)
             for g in range(2):
                 nc.tensor.matmul_mx(
                     out=bank[:],
@@ -328,155 +303,184 @@ def tile_koopman_step_readout_f7_kernel(
             half = res[row][:, h * S : (h + 1) * S]
             nc.vector.tensor_tensor(half, live["y", row, h][:], half, ALU.add)
 
+        def o_copy(row, h):
+            nc.scalar.copy(
+                out=res[row][:, h * S : (h + 1) * S].rearrange("p (m t) -> p m t", t=4),
+                in_=live["o", row, h][:].rearrange("p (t m) -> p m t", t=4),
+            )
+
         def store(row):
             nc.sync.dma_start(out=out[row * P : (row + 1) * P, :], in_=res[row][:])
 
         def store_half(row, h):
             nc.sync.dma_start(out=out[row * P : (row + 1) * P, h * S : (h + 1) * S], in_=res[row][:, h * S : (h + 1) * S])
 
-        for t in range(4):
-            ws_permute(t)
-        for row in range(2):
-            x_transpose(row)
-            x_copy(row)
+        warm_up(3)
+        x_transpose(0)
+        x_copy(0)
+        warm_up(1)
+        x_transpose(1)
+        x_copy(1)
+        vec_transpose()
         x_transpose(2)
-        x_copy_v(2)
-        w_permute(0, slice(0, 1))
+        x_copy(2)
+        warm_up(1)
         x_transpose(3)
         x_copy(3)
+        ws_permute(0)
+        vec_copy()
+        vec_prepare()
+        load_v()
+        ws_permute(1)
+        w_permute(0, 1)
+        warm_up(1, True)
         x_quant(0, 0)
         x_quant(0, 1)
-        w_permute(0, slice(1, 2))
-        lift_all(0)
-        w_permute(1, slice(0, 2))
-        act(0)
+        w_permute(0, 0)
+        diag_build()
+        for part in (FREQ, DAMP, RE, IM):
+            lift(0, part)
+        ws_permute(2)
+        ws_permute(3)
+        w_permute(1, 1)
+        w_permute(1, 0)
+        w_permute(2, 1)
+        w_permute(2, 0)
+        for kind in "fdcsri":
+            act(0, kind)
+        for part in (FREQ, DAMP, RE, IM):
+            lift(1, part)
+        v1(0)
+        w_permute(3, 1)
+        w_permute(3, 0)
+        v2(0)
+        for kind in "fdcsri":
+            act(1, kind)
+        for part in (FREQ, DAMP, RE, IM):
+            lift(2, part)
         x_transpose(4)
         x_transpose(5)
-        lift_all(1)
-        w_permute(2, slice(0, 2))
-        x_copy(4)
-        v1(0)
-        w_permute(3, slice(0, 2))
-        v2(0)
-        act(1)
-        x_copy(5)
-        x_transpose(6)
-        lift_all(2)
-        x_transpose(7)
         v1(1)
         v3(0)
         v2(1)
-        x_copy(6)
-        act(2)
-        lift_all(3)
-        x_copy_v(7)
+        for kind in "fdcsri":
+            act(2, kind)
+        for part in (FREQ, DAMP, RE, IM):
+            lift(3, part)
+        x_copy(4)
+        x_copy(5)
+        x_transpose(6)
+        x_transpose(7)
+        r_mm(0, 0)
+        r_mm(0, 1)
         v1(2)
         v3(1)
         v2(2)
-        act(3)
-        x_quant(1, 0)
-        x_quant(1, 1)
-        offset_mm()
-        lift_all(4)
+        for kind in "fdcsri":
+            act(3, kind)
+        o_copy(0, 0)
+        o_copy(0, 1)
+        x_copy(6)
+        x_copy(7)
+        r_mm(1, 0)
+        r_mm(1, 1)
         v1(3)
         v3(2)
         v2(3)
-        offset_copy()
-        act(4)
+        x_quant(1, 0)
+        x_quant(1, 1)
+        v3(3)
+        for part in (FREQ, DAMP, RE, IM):
+            lift(4, part)
+        o_copy(1, 0)
+        o_copy(1, 1)
+        z_step(0, 0, 0, S)
+        for kind in "fdcsri":
+            act(4, kind)
+        r_mm(2, 0)
+        r_mm(2, 1)
+        for part in (FREQ, DAMP, RE, IM):
+            lift(5, part)
+        o_copy(2, 0)
+        o_copy(2, 1)
+        z_step(0, 1, 0, S)
+        z_quant(0, 0, 0, S)
+        v1(4)
+        z_quant(0, 1, 0, S)
+        v2(4)
+        for kind in "fdcsri":
+            act(5, kind)
+        r_mm(3, 0)
+        r_mm(3, 1)
+        y_mm(0, 0)
+        y_mm(0, 1)
+        for part in (FREQ, DAMP, RE, IM):
+            lift(6, part)
+        o_copy(3, 0)
+        o_copy(3, 1)
+        v1(5)
+        v3(4)
+        y_add(0, 0)
+        store_half(0, 0)
+        v2(5)
+        y_add(0, 1)
+        store_half(0, 1)
+        v3(5)
+        for kind in "fdcsri":
+            act(6, kind)
         r_mm(4, 0)
         r_mm(4, 1)
-        lift_all(5)
-        v3(3)
-        act(5)
-        v1(4)
+        y_mm(1, 0)
+        y_mm(1, 1)
+        for part in (FREQ, DAMP, RE, IM):
+            lift(7, part)
         o_copy(4, 0)
         o_copy(4, 1)
-        lift_all(6)
-        r_mm(5, 0)
-        r_mm(5, 1)
-        z_step(0, 0, 0, S)
-        z_step(0, 1, 0, S)
-        v2(4)
-        z_quant(0, 0, 0, S)
-        z_quant(0, 1, 0, S)
-        v1(5)
-        o_copy(5, 0)
-        o_copy(5, 1)
-        r_mm(6, 0)
-        r_mm(6, 1)
-        v3(4)
-        v2(5)
-        act(6)
-        lift_all(7)
         v1(6)
-        v3(5)
+        y_add(1, 0)
+        store_half(1, 0)
         v2(6)
-        yt_mm(0)
-        yt_mm(1)
-        act(7)
-        v1(7)
+        y_add(1, 1)
+        store_half(1, 1)
         v3(6)
+        for kind in "fdcsri":
+            act(7, kind)
+        y_mm(2, 0)
+        y_mm(2, 1)
+        for h in range(2):
+            r_mm(5, h)
+            o_copy(5, h)
+        v1(7)
+        y_add(2, 0)
+        store_half(2, 0)
         v2(7)
+        y_add(2, 1)
+        store_half(2, 1)
         v3(7)
-
-        for j in range(8):
-            yt_copy(j)
-            if j < 6:
-                yt_mm(j + 2)
-            if j == 4:
-                o_mm(0, 0)
-            if j == 5:
-                o_mm(1, 0)
-        o_copy(6, 0)
-        o_copy(6, 1)
-        o_mm(2, 0)
-        r_mm(7, 0)
-        r_mm(7, 1)
-        o_copy(0, 0)
-        o_mm(3, 0)
-        o_copy(1, 0)
-        o_copy(7, 0)
-        o_copy(7, 1)
+        y_mm(3, 0)
+        y_mm(3, 1)
+        for row in range(6, 8):
+            for h in range(2):
+                r_mm(row, h)
+                o_copy(row, h)
+        y_add(3, 0)
+        store_half(3, 0)
         z_step(1, 0, 0, 256)
         z_step(1, 1, 0, 256)
         z_quant(1, 0, 0, 256)
-        z_step(1, 0, 256, 512)
+        y_add(3, 1)
+        store_half(3, 1)
         z_quant(1, 1, 0, 256)
+        z_step(1, 0, 256, 512)
         z_step(1, 1, 256, 512)
         z_quant(1, 0, 256, 512)
         z_quant(1, 1, 256, 512)
-        o_copy(2, 0)
-        o_mm(0, 1)
-        o_copy(3, 0)
-        o_copy(0, 1)
-        store(0)
-        y_mm(4, 0)
-        y_mm(4, 1)
-        o_mm(1, 1)
-        o_copy(1, 1)
-        store(1)
-        y_add(4, 0)
-        y_mm(5, 0)
-        y_add(4, 1)
-        store(4)
-        y_mm(5, 1)
-        y_add(5, 0)
-        y_mm(6, 0)
-        y_add(5, 1)
-        store(5)
-        y_mm(6, 1)
-        o_mm(2, 1)
-        o_copy(2, 1)
-        store(2)
-        y_add(6, 0)
-        y_mm(7, 0)
-        y_add(6, 1)
-        store(6)
-        y_mm(7, 1)
-        o_mm(3, 1)
-        o_copy(3, 1)
-        store(3)
-        y_add(7, 0)
-        store_half(7, 0)
-        y_add(7, 1)
-        store_half(7, 1)
+        for row in (4, 5):
+            for h in range(2):
+                y_mm(row, h)
+        for row in range(4, 8):
+            for h in range(2):
+                y_add(row, h)
+                store_half(row, h)
+                if row < 6:
+                    y_mm(row + 2, h)

import math
from contextlib import ExitStack

import concourse.mybir as mybir
from concourse.masks import make_identity

F32 = mybir.dt.float32
BF16 = mybir.dt.bfloat16
I32 = mybir.dt.int32
U32 = mybir.dt.uint32
U8 = mybir.dt.uint8
E4M3X4 = mybir.dt.float8_e4m3fn_x4
E2M1X4 = mybir.dt.float4_e2m1fn_x4
ACT = mybir.ActivationFunctionType
ALU = mybir.AluOpType

P = 128
ROWS = 1024
CH = 1024
MODES = 512
LIFT = 4 * MODES
S = 512
FLOPS = 2 * ROWS * CH * LIFT + 2 * ROWS * 2 * MODES * CH

RE, IM, FREQ, DAMP = 0, 1, 2, 3


def tile_koopman_step_readout_f7_kernel(
    tc, x, lift_words, lift_scales, bias, omega, nu, amp, modes_words, modes_scales, unit, offset, out
):
    nc = tc.nc
    with ExitStack() as ctx:
        keep = ctx.enter_context(tc.tile_pool(name="keep", bufs=1))
        work = ctx.enter_context(tc.tile_pool(name="work", bufs=3))
        psum = ctx.enter_context(tc.psum_pool(name="psum", bufs=1))
        ctx.enter_context(tc.manual_schedule())

        vec_rows = keep.tile([P, MODES], BF16, name="vec_rows", align_bytes=64)
        vec = keep.tile([P, 4, 16], F32, name="vec")
        off_r = keep.tile([1, CH], BF16, name="off_r", align_bytes=64)
        off_p = keep.tile([P, 2, 4, P], BF16, name="off_p", align_bytes=64)
        ones = keep.tile([P, P], BF16, name="ones", align_bytes=64)
        warm = keep.tile([P, 1], F32, name="warm")
        warm_b = keep.tile([P, S], BF16, name="warm_b", align_bytes=64)
        ident = keep.tile([P, P], F32, name="ident", align_bytes=64)
        ident_b = keep.tile([P, P], BF16, name="ident_b", align_bytes=64)
        diag = keep.tile([P, 8, P], BF16, name="diag", align_bytes=64)
        half_b = keep.tile([P, 4], F32, name="half_b")
        half_amp = keep.tile([P, 4], F32, name="half_amp")
        nsign = keep.tile([P, 4], F32, name="nsign")
        cos_s = keep.tile([P, 4], F32, name="cos_s")
        cos_b = keep.tile([P, 4], F32, name="cos_b")

        w_raw = keep.tile([P, 2, 2, LIFT], U8, name="w_raw", align_bytes=64)
        w_perm = keep.tile([P, 4, 2, 2, LIFT // 4], U8, name="w_perm", align_bytes=64)
        ws_raw = keep.tile([P, 2, LIFT], U8, name="ws_raw", align_bytes=64)
        ws_perm = keep.tile([P, 4, 2, LIFT // 4], U8, name="ws_perm", align_bytes=64)
        v_codes = keep.tile([P, 2, CH * 4], U8, name="v_codes", align_bytes=64)
        v_scales = keep.tile([P, 2, CH], U8, name="v_scales", align_bytes=64)

        x_rows = []
        x_tiles = [keep.tile([P, n, CH], BF16, name="x%d" % k, align_bytes=64) for k, n in enumerate((1, 1, 2, 2, 2))]
        for tile in x_tiles:
            x_rows += [tile[:, i, :] for i in range(tile.shape[1])]

        def load_x(k):
            n = x_tiles[k].shape[1]
            row = (0, 1, 2, 4, 6)[k]
            src = x[row * P : (row + n) * P, :].rearrange("(i p) c -> p i c", p=P)
            nc.sync.dma_start(out=x_tiles[k][:], in_=src)

        def load_ws(r):
            src = lift_scales.bitcast(I32).rearrange("g (a r) n -> r a g n", r=4)
            nc.sync.dma_start(out=ws_raw[r:P:32, :, :].bitcast(I32), in_=src[r])

        def load_w(half):
            src = lift_words.bitcast(I32).rearrange("g p (h n) -> h p g n", h=2)
            nc.sync.dma_start(out=w_raw[:, half].bitcast(I32), in_=src[half])

        nc.vector.memset(warm[:], 0.0)
        nc.vector.memset(warm_b[:].bitcast(I32), 0)
        nc.vector.memset(vec_rows[:].bitcast(I32), 0)
        nc.vector.memset(ws_raw[:].rearrange("p g n -> p (g n)").bitcast(I32), 0)
        make_identity(nc, ident[:])
        nc.scalar.dma_start(out=vec_rows[0:4, :], in_=bias.rearrange("(a n) -> a n", a=4))
        nc.scalar.dma_start(out=vec_rows[4:5, :], in_=omega.unsqueeze(0))
        nc.scalar.dma_start(out=vec_rows[5:6, :], in_=nu.unsqueeze(0))
        nc.gpsimd.dma_start(out=vec_rows[6:7, :], in_=amp.unsqueeze(0))
        nc.gpsimd.dma_start(out=vec_rows[7:9, :], in_=unit.rearrange("(a n) -> a n", a=2))
        nc.scalar.activation(warm[:], warm[:], ACT.Silu)
        load_x(0)
        load_x(1)
        load_x(2)
        for r in range(4):
            load_ws(r)
        load_w(1)
        load_w(0)
        load_x(3)
        load_x(4)
        nc.vector.tensor_copy(out=ident_b[:], in_=ident[:])

        def warm_up(n, late=False):
            bank = psum.tile([P, S], F32, name="y", bufs=2)
            rhs = xg[0][:, 0, 3 * P : S, :].rearrange("p s j -> p (s j)") if late else warm_b[:]
            for i in range(n):
                nc.tensor.matmul(bank[:], lhsT=warm_b[:, 0:P], rhs=rhs, start=True, stop=True)

        def vec_transpose():
            bank = psum.tile([P, 4, P], BF16, name="y", bufs=2)
            for t in range(4):
                nc.tensor.transpose(bank[:, t, :], vec_rows[:, t : MODES : 4], ident_b[:])
            live["vec"] = bank

        def vec_copy():
            nc.vector.tensor_copy(out=vec[:], in_=live["vec"][:, :, 0:16])

        def vec_prepare():
            nc.gpsimd.tensor_scalar(half_b[:], vec[:, :, DAMP], 0.5, None, ALU.mult)
            nc.gpsimd.tensor_scalar(nsign[:], vec[:, :, 4], 0.0, -2.0, ALU.is_ge, ALU.mult)
            nc.gpsimd.tensor_scalar(nsign[:], nsign[:], 1.0, None, ALU.add)
            nc.gpsimd.tensor_tensor(cos_s[:], nsign[:], vec[:, :, 5], ALU.mult)
            nc.gpsimd.tensor_tensor(cos_b[:], nsign[:], vec[:, :, 4], ALU.mult)
            nc.gpsimd.tensor_scalar(cos_b[:], cos_b[:], math.pi / 2, None, ALU.add)
            nc.gpsimd.tensor_scalar(half_amp[:], vec[:, :, 6], 0.5, None, ALU.mult)

        def diag_build():
            for g in range(2):
                for t in range(4):
                    nc.scalar.activation(diag[:, 4 * g + t, :], ident[:], ACT.Copy, scale=vec[:, t, 7 + g : 8 + g])

        def load_v():
            nc.gpsimd.memset(v_scales[:].rearrange("p g n -> p (g n)").bitcast(I32), 0)
            nc.gpsimd.memset(ones[:], 1.0)
            nc.gpsimd.memset(off_p[:], 0.0)
            src = modes_scales.bitcast(I32).rearrange("g (a r) n -> r a g n", r=4)
            for r in range(4):
                nc.sync.dma_start(out=v_scales[r:P:32, :, :].bitcast(I32), in_=src[r])
            nc.sync.dma_start(out=off_r[0:1, :], in_=offset.unsqueeze(0))
            for g in range(2):
                nc.sync.dma_start(out=v_codes[:, g, :].bitcast(I32), in_=modes_words[g].rearrange("p n t -> p (n t)").bitcast(I32))
            nc.gpsimd.tensor_scalar(
                off_p[0:1], off_r[0:1, :].rearrange("o (g m t) -> o g t m", g=2, t=4), 1.0, 0.0, ALU.mult, ALU.add
            )

        xg = [keep.tile([P, 2, S, 4], BF16, name="xg%d" % c, align_bytes=64) for c in range(2)]
        xc = [keep.tile([P, 2, S], U32, name="xc%d" % c, align_bytes=64) for c in range(2)]
        xs = [keep.tile([P, 2, S], U8, name="xs%d" % c, align_bytes=64) for c in range(2)]
        zg = [keep.tile([P, 2, S, 4], BF16, name="zg%d" % c, align_bytes=64) for c in range(2)]
        zc = [keep.tile([P, 2, S], U32, name="zc%d" % c, align_bytes=64) for c in range(2)]
        zs = [keep.tile([P, 2, S], U8, name="zs%d" % c, align_bytes=64) for c in range(2)]
        res = [keep.tile([P, CH], F32, name="res%d" % row, align_bytes=64) for row in range(8)]
        live = {}

        def x_transpose(row):
            words = x_rows[row].bitcast(F32)
            bank = psum.tile([P, 4, P], F32, name="o" if row < 4 else "y", bufs=2)
            for g in range(2):
                for u in range(2):
                    nc.tensor.transpose(bank[:, 2 * g + u, :], words[:, 256 * g + u : 256 * (g + 1) : 2], ident[:])
            live["xt", row] = bank

        def x_copy(row):
            c, r = divmod(row, 4)
            dst = xg[c][:].rearrange("p g s j -> p (g s j)").bitcast(F32).rearrange("p (g s u) -> p g s u", g=2, u=2)
            src = live["xt", row][:].rearrange("p (g u) s -> p g s u", u=2)
            nc.scalar.copy(out=dst[:, :, r * P : (r + 1) * P, :], in_=src)

        def x_copy_v(row):
            c, r = divmod(row, 4)
            dst = xg[c][:].rearrange("p g s j -> p (g s j)").bitcast(F32).rearrange("p (g s u) -> p g s u", g=2, u=2)
            src = live["xt", row][:].rearrange("p (g u) s -> p g s u", u=2)
            nc.vector.tensor_copy(out=dst[:, :, r * P : (r + 1) * P, :], in_=src)

        def x_quant(c, g):
            nc.vector.quantize_mx(
                out=xc[c][:, g, :].bitcast(E4M3X4),
                scales=xs[c][:, g, :],
                in_=xg[c][:, g, :, :].rearrange("p s j -> p (s j)"),
            )

        def w_permute(t, half):
            src = w_raw[:, half].rearrange("p g (n t b) -> p t g n b", t=4, b=2)
            dst = w_perm[:, t, half].rearrange("p g (n b) -> p g n b", b=2)
            nc.vector.tensor_copy(out=dst, in_=src[:, t])

        def ws_permute(t):
            src = ws_raw[:].rearrange("p g (n t) -> p t g n", t=4)
            nc.vector.tensor_copy(out=ws_perm[:, t], in_=src[:, t])

        def lift(u, part):
            c, t = divmod(u, 4)
            bank = psum.tile([P, S], F32, name="h%d" % part)
            for g in range(2):
                nc.tensor.matmul_mx(
                    out=bank[:],
                    lhsT=w_perm[:, t, part // 2, g, 2 * P * (part % 2) : 2 * P * (part % 2 + 1)].bitcast(E2M1X4),
                    lhsT_scale=ws_perm[:, t, g, P * part : P * (part + 1)],
                    rhs=xc[c][:, g, :].bitcast(E4M3X4),
                    rhs_scale=xs[c][:, g, :],
                    start=(g == 0),
                    stop=(g == 1),
                )
            live["h", u, part] = bank

        def act(u, kind):
            t = u % 4
            if kind == "f":
                live["f", u] = work.tile([P, S], F32, name="tf", bufs=2)
                nc.scalar.activation(live["f", u][:], live["h", u, FREQ][:], ACT.Tanh, bias=vec[:, t, FREQ : FREQ + 1])
            elif kind == "d":
                live["d", u] = work.tile([P, S], F32, name="td")
                nc.scalar.activation(live["d", u][:], live["h", u, DAMP][:], ACT.Tanh, bias=half_b[:, t : t + 1], scale=0.5)
            elif kind == "c":
                live["trig", u] = work.tile([P, 2, S], F32, name="trig")
                nc.scalar.activation(live["trig", u][:, 0, :], live["f", u][:], ACT.Sin, bias=cos_b[:, t : t + 1], scale=cos_s[:, t : t + 1])
            elif kind == "s":
                nc.scalar.activation(live["trig", u][:, 1, :], live["f", u][:], ACT.Sin, bias=vec[:, t, 4:5], scale=vec[:, t, 5:6])
            elif kind == "r":
                live["r", u] = work.tile([P, S], F32, name="tre")
                nc.scalar.activation(live["r", u][:], live["h", u, RE][:], ACT.Tanh, bias=vec[:, t, RE : RE + 1])
            else:
                live["i", u] = work.tile([P, S], F32, name="tim")
                nc.scalar.activation(live["i", u][:], live["h", u, IM][:], ACT.Tanh, bias=vec[:, t, IM : IM + 1])

        def v1(u):
            td, trig = live["d", u], live["trig", u]
            rot = work.tile([P, 2, S], F32, name="rot", bufs=2)
            nc.vector.scalar_tensor_tensor(
                out=rot[:], in0=td[:].unsqueeze(1).to_broadcast([P, 2, S]), scalar=1.0, in1=trig[:], op0=ALU.add, op1=ALU.mult
            )
            live["rot", u] = rot

        def v23(u, which):
            t = u % 4
            if ("p", u // 4, which) not in live:
                live["p", u // 4, which] = work.tile([P, 4, 2, S], F32, name="p%d" % which, bufs=1)
            src = live["ri"[which], u]
            nc.vector.scalar_tensor_tensor(
                out=live["p", u // 4, which][:, t, :, :],
                in0=src[:].unsqueeze(1).to_broadcast([P, 2, S]),
                scalar=half_amp[:, t : t + 1],
                in1=live["rot", u][:],
                op0=ALU.mult,
                op1=ALU.mult,
            )

        def v2(u):
            v23(u, 0)

        def v3(u):
            v23(u, 1)

        def z_step(c, part, lo, hi):
            a = live["p", c, 0][:, :, part, lo:hi].rearrange("p t (c i) -> p c t i", i=4)
            b = live["p", c, 1][:, :, 1 - part, lo:hi].rearrange("p t (c i) -> p c t i", i=4)
            dst = zg[c][:, part, lo:hi, :].rearrange("p (c i) t -> p c t i", i=4)
            nc.vector.tensor_tensor(dst, a, b, ALU.subtract if part == 0 else ALU.add)

        def z_quant(c, part, lo, hi):
            nc.vector.quantize_mx(
                out=zc[c][:, part, lo:hi].bitcast(E4M3X4),
                scales=zs[c][:, part, lo:hi],
                in_=zg[c][:, part, lo:hi, :].rearrange("p s j -> p (s j)"),
            )

        def add_x(bank, row, g, start, stop):
            c, r = divmod(row, 4)
            cols = bank[:].rearrange("p (t m) -> p t m", t=4)
            for t in range(4):
                nc.tensor.matmul(
                    cols[:, t, :],
                    lhsT=xg[c][:, g, r * P : (r + 1) * P, t],
                    rhs=diag[:, 4 * g + t, :],
                    start=(start and t == 0),
                    stop=(stop and t == 3),
                )

        def offset_mm(bank, h):
            nc.tensor.matmul(bank[:], lhsT=ones[:], rhs=off_p[:, h].rearrange("p t m -> p (t m)"), start=True, stop=False)

        def r_mm(row, h):
            bank = psum.tile([P, S], F32, name="o", bufs=2)
            offset_mm(bank, h)
            add_x(bank, row, h, False, True)
            live["o", row, h] = bank

        def y_mm(row, h):
            c, r = divmod(row, 4)
            bank = psum.tile([P, S], F32, name="o" if row in (5, 7) else "y", bufs=2)
            for g in range(2):
                nc.tensor.matmul_mx(
                    out=bank[:],
                    lhsT=zc[c][:, g, r * P : (r + 1) * P].bitcast(E4M3X4),
                    lhsT_scale=zs[c][:, g, r * P : (r + 1) * P],
                    rhs=v_codes[:, g, 4 * h * S : 4 * (h + 1) * S].bitcast(E4M3X4),
                    rhs_scale=v_scales[:, g, h * S : (h + 1) * S],
                    start=(g == 0),
                    stop=(g == 1),
                )
            live["y", row, h] = bank

        def y_add(row, h):
            half = res[row][:, h * S : (h + 1) * S]
            nc.vector.tensor_tensor(half, live["y", row, h][:], half, ALU.add)

        def o_copy(row, h):
            nc.scalar.copy(
                out=res[row][:, h * S : (h + 1) * S].rearrange("p (m t) -> p m t", t=4),
                in_=live["o", row, h][:].rearrange("p (t m) -> p m t", t=4),
            )

        def store(row):
            nc.sync.dma_start(out=out[row * P : (row + 1) * P, :], in_=res[row][:])

        def store_half(row, h):
            nc.sync.dma_start(out=out[row * P : (row + 1) * P, h * S : (h + 1) * S], in_=res[row][:, h * S : (h + 1) * S])

        warm_up(3)
        x_transpose(0)
        x_copy(0)
        warm_up(1)
        x_transpose(1)
        x_copy(1)
        vec_transpose()
        x_transpose(2)
        x_copy(2)
        warm_up(1)
        x_transpose(3)
        x_copy(3)
        ws_permute(0)
        vec_copy()
        vec_prepare()
        load_v()
        ws_permute(1)
        w_permute(0, 1)
        warm_up(1, True)
        x_quant(0, 0)
        x_quant(0, 1)
        w_permute(0, 0)
        diag_build()
        for part in (FREQ, DAMP, RE, IM):
            lift(0, part)
        ws_permute(2)
        ws_permute(3)
        w_permute(1, 1)
        w_permute(1, 0)
        w_permute(2, 1)
        w_permute(2, 0)
        for kind in "fdcsri":
            act(0, kind)
        for part in (FREQ, DAMP, RE, IM):
            lift(1, part)
        v1(0)
        w_permute(3, 1)
        w_permute(3, 0)
        v2(0)
        for kind in "fdcsri":
            act(1, kind)
        for part in (FREQ, DAMP, RE, IM):
            lift(2, part)
        x_transpose(4)
        x_transpose(5)
        v1(1)
        v3(0)
        v2(1)
        for kind in "fdcsri":
            act(2, kind)
        for part in (FREQ, DAMP, RE, IM):
            lift(3, part)
        x_copy(4)
        x_copy(5)
        x_transpose(6)
        x_transpose(7)
        r_mm(0, 0)
        r_mm(0, 1)
        v1(2)
        v3(1)
        v2(2)
        for kind in "fdcsri":
            act(3, kind)
        o_copy(0, 0)
        o_copy(0, 1)
        x_copy(6)
        x_copy(7)
        r_mm(1, 0)
        r_mm(1, 1)
        v1(3)
        v3(2)
        v2(3)
        x_quant(1, 0)
        x_quant(1, 1)
        v3(3)
        for part in (FREQ, DAMP, RE, IM):
            lift(4, part)
        o_copy(1, 0)
        o_copy(1, 1)
        z_step(0, 0, 0, S)
        for kind in "fdcsri":
            act(4, kind)
        r_mm(2, 0)
        r_mm(2, 1)
        for part in (FREQ, DAMP, RE, IM):
            lift(5, part)
        o_copy(2, 0)
        o_copy(2, 1)
        z_step(0, 1, 0, S)
        z_quant(0, 0, 0, S)
        v1(4)
        z_quant(0, 1, 0, S)
        v2(4)
        for kind in "fdcsri":
            act(5, kind)
        r_mm(3, 0)
        r_mm(3, 1)
        y_mm(0, 0)
        y_mm(0, 1)
        for part in (FREQ, DAMP, RE, IM):
            lift(6, part)
        o_copy(3, 0)
        o_copy(3, 1)
        v1(5)
        v3(4)
        y_add(0, 0)
        store_half(0, 0)
        v2(5)
        y_add(0, 1)
        store_half(0, 1)
        v3(5)
        for kind in "fdcsri":
            act(6, kind)
        r_mm(4, 0)
        r_mm(4, 1)
        y_mm(1, 0)
        y_mm(1, 1)
        for part in (FREQ, DAMP, RE, IM):
            lift(7, part)
        o_copy(4, 0)
        o_copy(4, 1)
        v1(6)
        y_add(1, 0)
        store_half(1, 0)
        v2(6)
        y_add(1, 1)
        store_half(1, 1)
        v3(6)
        for kind in "fdcsri":
            act(7, kind)
        y_mm(2, 0)
        y_mm(2, 1)
        for h in range(2):
            r_mm(5, h)
            o_copy(5, h)
        v1(7)
        y_add(2, 0)
        store_half(2, 0)
        v2(7)
        y_add(2, 1)
        store_half(2, 1)
        v3(7)
        y_mm(3, 0)
        y_mm(3, 1)
        for row in range(6, 8):
            for h in range(2):
                r_mm(row, h)
                o_copy(row, h)
        y_add(3, 0)
        store_half(3, 0)
        z_step(1, 0, 0, 256)
        z_step(1, 1, 0, 256)
        z_quant(1, 0, 0, 256)
        y_add(3, 1)
        store_half(3, 1)
        z_quant(1, 1, 0, 256)
        z_step(1, 0, 256, 512)
        z_step(1, 1, 256, 512)
        z_quant(1, 0, 256, 512)
        z_quant(1, 1, 256, 512)
        for row in (4, 5):
            for h in range(2):
                y_mm(row, h)
        for row in range(4, 8):
            for h in range(2):
                y_add(row, h)
                store_half(row, h)
                if row < 6:
                    y_mm(row + 2, h)
